import numpy as np
import ml_dtypes


def mxq(x, axis, fmt="e4m3"):
    dtype, down = {"e4m3": (ml_dtypes.float8_e4m3fn, 7), "e5m2": (ml_dtypes.float8_e5m2, 14)}[fmt]
    v = np.moveaxis(np.asarray(x, np.float32).astype(ml_dtypes.bfloat16).astype(np.float64), axis, -1)
    blocks = v.reshape(v.shape[:-1] + (-1, 32))
    amax = np.abs(blocks).max(-1, keepdims=True)
    byte = np.maximum(np.where(amax > 0, np.frexp(amax)[1] - 1 + 127, 0) - down, 1)
    scale = np.exp2(byte - 127.0)
    codes = (blocks / scale).astype(np.float32).astype(dtype).astype(np.float64)
    return np.moveaxis((codes * scale).reshape(v.shape), -1, axis)


WIDE = False


def mx_kscale(k):
    if not WIDE:
        return np.ones(k)
    levels = np.array([10, -10, 5, -5, 0])
    if k % 512:
        return np.exp2(np.random.permutation(np.resize(levels, k // 32))).repeat(32)
    a = np.empty((k // 512, 16))
    for p in range(k // 512):
        a[p, :8] = np.random.permutation(np.resize(levels, 8))
        for g in range(8):
            far = levels[np.abs(levels - a[p, g]) >= 10]
            a[p, g + 8] = far[np.random.randint(len(far))]
    return np.exp2(a.ravel()).repeat(32)


def f64(x):
    return np.asarray(x).astype(np.float64)


def striped(idx):
    return np.tile(idx.reshape(-1, 16).T, (8, 1)).astype(np.uint16)


def unstriped(offs):
    return offs[:16].T.reshape(-1).astype(np.int64)


def striped8(idx):
    return np.concatenate([x.reshape(-1, 16).T for x in idx]).astype(np.uint16)


def runs(offs, k):
    lists = np.stack([offs[16 * r : 16 * r + 16].T.reshape(-1) for r in range(8)]).astype(np.int64)
    return lists[np.arange(k) % 512 // 64]


def pack_weight(w):
    k, n = w.shape
    w = f64(np.asarray(w, np.float32).astype(ml_dtypes.bfloat16)).reshape(k // 32, 32, n)
    amax = np.abs(w).max(1)
    byte = np.clip(np.where(amax > 0, np.frexp(amax)[1] - 1 + 127 - 7, 1), 1, 254)
    scaled = (w * np.exp2(127.0 - byte)[:, None, :]).reshape(k, n).astype(np.float32)
    words = np.ascontiguousarray(scaled.reshape(k // 512, 128, 4, n).transpose(0, 1, 3, 2)).astype(ml_dtypes.float8_e4m3fn).view(np.uint8)
    return words, np.ascontiguousarray(byte.astype(np.uint8).reshape(k // 512, 16, n))


def unpack_weight(words, scales):
    g, p, n, _ = words.shape
    vals = np.ascontiguousarray(words).view(ml_dtypes.float8_e4m3fn).astype(np.float64) * np.repeat(np.exp2(scales.astype(np.float64) - 127.0), 8, axis=1)[..., None]
    return vals.transpose(0, 1, 3, 2).reshape(g * 512, n)


E2M1 = np.array([0.0, 0.5, 1.0, 1.5, 2.0, 3.0, 4.0, 6.0, -0.0, -0.5, -1.0, -1.5, -2.0, -3.0, -4.0, -6.0])


def pack_fp4(w):
    k, n = w.shape
    w = f64(np.asarray(w, np.float32).astype(ml_dtypes.bfloat16)).reshape(k // 32, 32, n)
    amax = np.abs(w).max(1)
    mant, ex = np.frexp(amax / 6.0)
    byte = np.clip(np.where(amax > 0, np.where(mant > 0.5, ex, ex - 1) + 127, 1), 1, 254)
    scaled = (w * np.exp2(127.0 - byte)[:, None, :]).reshape(k, n).astype(np.float32)
    c = np.ascontiguousarray(scaled.reshape(k // 512, 128, 4, n).transpose(0, 1, 3, 2)).astype(ml_dtypes.float4_e2m1fn).view(np.uint8) & 0xF
    words = (c[..., 0::2] | (c[..., 1::2] << 4)).reshape(k // 512, 128, 2 * n)
    return np.ascontiguousarray(words), np.ascontiguousarray(byte.astype(np.uint8).reshape(k // 512, 16, n))


def unpack_fp4(words, scales):
    g, _, n = scales.shape
    words = np.ascontiguousarray(words).reshape(g, 128, n, 2)
    nib = np.empty((g, 128, n, 4), np.uint8)
    nib[..., 0::2] = words & 0xF
    nib[..., 1::2] = words >> 4
    vals = E2M1[nib] * np.repeat(np.exp2(scales.astype(np.float64) - 127.0), 8, axis=1)[..., None]
    return vals.transpose(0, 1, 3, 2).reshape(g * 512, n)


def sigmoid(v):
    return 1.0 / (1.0 + np.exp(-np.maximum(v, -700.0)))

def planes(y):
    n, m = y.shape
    v = y.astype(np.float32).astype(ml_dtypes.bfloat16).astype(np.float64).reshape(n // 32, 32, m)
    top = np.abs(v).max(1)
    byte = np.clip(np.where(top > 0, np.frexp(top)[1] - 1 + 127 - 7, 1), 1, 254)
    codes = (v * np.exp2(127.0 - byte)[:, None, :]).reshape(n, m).astype(np.float32).astype(ml_dtypes.float8_e4m3fn).view(np.uint8)
    words = codes.reshape(n // 512, 128, 4, m).transpose(0, 1, 3, 2)
    return np.ascontiguousarray(words), np.ascontiguousarray(byte.astype(np.uint8).reshape(n // 512, 16, m))


K, T, S, N, H, J = 512, 2048, 512, 512, 512, 512


def setup_inputs():
    n = np.random.standard_normal
    s = mx_kscale(K)[:, None]
    u = mx_kscale(H)
    packed_xT = pack_weight(n((K, T)) * s)
    packed_w1 = pack_fp4(n((K, H)) / np.sqrt(K) / s)
    packed_w2 = pack_fp4(n((H, N)) / np.sqrt(H) / u[:, None])
    packed_w3 = pack_fp4(n((H, N)) / np.sqrt(H) / u[:, None])
    return {
        "x_words": packed_xT[0],
        "x_scales": packed_xT[1],
        "w1_words": packed_w1[0],
        "w1_scales": packed_w1[1],
        "tab": n((H, J)).astype(np.float32),
        "gn": (np.random.uniform(0.5, 1.5, (H, 1)) * u[:, None]).astype(np.float32),
        "w2_words": packed_w2[0],
        "w2_scales": packed_w2[1],
        "gm": (np.random.uniform(0.5, 1.5, (H, 1)) * u[:, None]).astype(np.float32),
        "w3_words": packed_w3[0],
        "w3_scales": packed_w3[1],
        "offs": striped(np.random.permutation(T)[:S]),
        "n1": striped8(np.random.randint(0, J, (8, S))),
        "n2": striped8(np.stack([np.random.permutation(S) for _ in range(8)])),
        "n3": striped8(np.stack([np.random.permutation(S) for _ in range(8)])),
        "n4": striped8(np.stack([np.random.permutation(S) for _ in range(8)])),
        "n5": striped8(np.stack([np.random.permutation(S) for _ in range(8)])),
        "n6": striped8(np.stack([np.random.permutation(S) for _ in range(8)])),
    }


def reference(x_words, x_scales, w1_words, w1_scales, tab, gn, w2_words, w2_scales, gm, w3_words, w3_scales, offs, n1, n2, n3, n4, n5, n6):
    xq = unpack_weight(x_words, x_scales)[:, unstriped(offs)]
    y = unpack_fp4(w1_words, w1_scales).T @ xq
    z = f64(gn) * (np.abs(y - (y[np.arange(H)[:, None], runs(n2, H)]) - (f64(tab)[np.arange(H)[:, None], runs(n1, H)])))
    a = unpack_fp4(w2_words, w2_scales).T @ mxq(z, 0, "e4m3")
    ex = np.exp(y)
    z2 = f64(gm) * (np.log(ex + ex[np.arange(H)[:, None], runs(n3, H)]) - (y[np.arange(H)[:, None], runs(n4, H)]))
    b = unpack_fp4(w3_words, w3_scales).T @ mxq(z2, 0, "e4m3")
    out_0 = a + (sigmoid(b[np.arange(N)[:, None], runs(n6, N)] - b)) * (a[np.arange(N)[:, None], runs(n5, N)] - a)
    return (out_0,) + planes(out_0)

@@ -1,0 +1,288 @@
+from contextlib import ExitStack
+
+import concourse.mybir as mybir
+
+K, T, S, N, H, J = 512, 2048, 512, 512, 512, 512
+FLOPS = 3 * 2 * 512 * 512 * 512
+
+F32 = mybir.dt.float32
+BF16 = mybir.dt.bfloat16
+I32 = mybir.dt.int32
+U32 = mybir.dt.uint32
+U16 = mybir.dt.uint16
+U8 = mybir.dt.uint8
+FP8X4 = mybir.dt.float8_e4m3fn_x4
+FP4X4 = mybir.dt.float4_e2m1fn_x4
+ALU = mybir.AluOpType
+ACT = mybir.ActivationFunctionType
+
+P = 128
+PACK = 4
+QUADS = 4
+XPARTS = 4
+
+
+def tile_picked_forkpullbkinddlse_none_po_kernel(
+    tc, x_words, x_scales, w1_words, w1_scales, tab, gn, w2_words, w2_scales, gm, w3_words, w3_scales,
+    offs, n1, n2, n3, n4, n5, n6, out_0, out_1, out_2,
+):
+    nc = tc.nc
+    with ExitStack() as ctx:
+        keep = ctx.enter_context(tc.tile_pool(name="keep", bufs=1))
+        psum = ctx.enter_context(tc.psum_pool(name="psum", bufs=1))
+
+        def load_list(src, name):
+            t = keep.tile([P, S // 16], U16, name=name)
+            nc.sync.dma_start(t[:], src)
+            return t
+
+        def load_words(src, name):
+            t = keep.tile([P, 2 * N], U8, name=name)
+            nc.sync.dma_start(t[:].bitcast(I32), src[0].bitcast(I32))
+            return t
+
+        def load_scale_rows(dst, src):
+            for q in range(QUADS):
+                nc.sync.dma_start(dst[32 * q : 32 * q + 4, :].bitcast(I32), src[0][4 * q : 4 * q + 4, :].bitcast(I32))
+
+        def deal_words(raw, name):
+            t = keep.tile([P, PACK, P, 2], U8, name=name, align_bytes=64)
+            nc.vector.tensor_copy(t[:], raw[:].rearrange("p (m t b) -> p t m b", t=PACK, b=2))
+            return t
+
+        def layer(words, scales, t, codes, code_scales, bank):
+            acc = psum.tile([P, S], F32, name=bank, tag=bank)
+            nc.tensor.matmul_mx(
+                out=acc[:],
+                lhsT=words[:, t, :, :].rearrange("p m b -> p (m b)").bitcast(FP4X4),
+                lhsT_scale=scales[:, t, :],
+                rhs=codes[:].bitcast(FP8X4),
+                rhs_scale=code_scales[:],
+                start=True,
+                stop=True,
+            )
+            return acc
+
+        def windows(name):
+            return [keep.tile([P, 2 * S], F32, name="%s%d" % (name, t)) for t in range(PACK)]
+
+        def woven_src(planes, c0, c1):
+            return planes[:, :, c0:c1].rearrange("p t (c i) -> p c t i", i=4)
+
+        def woven_dst(packed, c0, c1):
+            return packed[:, c0:c1, :].rearrange("p (c i) t -> p c t i", i=4)
+
+        def quantize(codes, scales, packed, c0, c1):
+            nc.vector.quantize_mx(
+                out=codes[:, c0:c1].bitcast(FP8X4),
+                scales=scales[:, c0:c1],
+                in_=packed[:, c0:c1, :].rearrange("p j t -> p (j t)"),
+            )
+
+        lo, hi = slice(0, S), slice(S, 2 * S)
+        HALF = S // 2
+
+        xs_raw = keep.tile([P, T], U8, name="xs_raw")
+        w1s_raw = keep.tile([P, H], U8, name="w1s_raw")
+        w23s_raw = keep.tile([P, 2, N], U8, name="w23s_raw")
+        nc.gpsimd.memset(xs_raw[:].bitcast(I32), 0)
+        nc.gpsimd.memset(w1s_raw[:].bitcast(I32), 0)
+        nc.gpsimd.memset(w23s_raw[:].bitcast(I32), 0)
+        warm = keep.tile([P, 1], F32, name="warm")
+        nc.vector.memset(warm[:], 0.0)
+        nc.scalar.activation(warm[:], warm[:], ACT.Exp)
+
+        offs_t = load_list(offs, "offs_t")
+        w1_raw = load_words(w1_words, "w1_raw")
+        w2_raw = load_words(w2_words, "w2_raw")
+        w3_raw = load_words(w3_words, "w3_raw")
+        x_raw = keep.tile([P, T], I32, name="x_raw")
+        x_src = x_words[0].rearrange("p n t -> p (n t)").bitcast(I32)
+        for c0 in range(0, T, T // XPARTS):
+            nc.sync.dma_start(x_raw[:, c0 : c0 + T // XPARTS], x_src[:, c0 : c0 + T // XPARTS])
+        load_scale_rows(xs_raw[:], x_scales)
+        load_scale_rows(w1s_raw[:], w1_scales)
+        n3_t = load_list(n3, "n3_t")
+        load_scale_rows(w23s_raw[:, 0, :], w2_scales)
+        load_scale_rows(w23s_raw[:, 1, :], w3_scales)
+        gn_t = keep.tile([P, PACK], F32, name="gn_t")
+        gm_t = keep.tile([P, PACK], F32, name="gm_t")
+        nc.sync.dma_start(gm_t[:], gm.rearrange("(p t) o -> p (t o)", t=PACK))
+        n1_t = load_list(n1, "n1_t")
+        n2_t = load_list(n2, "n2_t")
+        nc.sync.dma_start(gn_t[:], gn.rearrange("(p t) o -> p (t o)", t=PACK))
+        n4_t = load_list(n4, "n4_t")
+        n5_t = load_list(n5, "n5_t")
+        n6_t = load_list(n6, "n6_t")
+
+        w1 = deal_words(w1_raw, "w1")
+        w2 = deal_words(w2_raw, "w2")
+        w3 = deal_words(w3_raw, "w3")
+        x_codes = keep.tile([P, S], U32, name="x_codes", align_bytes=64)
+        x_bytes = keep.tile([P, S], U8, name="x_bytes", align_bytes=64)
+        nc.vector.tensor_copy(x_codes[:], x_raw[:].bitcast(U32).indirect(offs_t[:]))
+        nc.vector.tensor_copy(x_bytes[:], xs_raw[:].indirect(offs_t[:]))
+        w1s = keep.tile([P, PACK, P], U8, name="w1s", align_bytes=64)
+        nc.vector.tensor_copy(w1s[:], w1s_raw[:].rearrange("p (m t) -> p t m", t=PACK))
+        w23s = keep.tile([P, 2, PACK, P], U8, name="w23s", align_bytes=64)
+        nc.vector.tensor_copy(w23s[:], w23s_raw[:].rearrange("p w (m t) -> p w t m", t=PACK))
+        w2s, w3s = w23s[:, 0, :, :], w23s[:, 1, :, :]
+
+        y_win = windows("y_win")
+        tab_win = windows("tab_win")
+        for t in range(PACK):
+            nc.vector.memset(y_win[t][:, hi], 0.0)
+        for t in range(PACK):
+            nc.vector.memset(tab_win[t][:, hi], 0.0)
+        ym_win = windows("ym_win")
+        a_win = windows("a_win")
+        b_win = windows("b_win")
+        soft = keep.tile([P, PACK, S], F32, name="soft")
+        z_planes = keep.tile([P, PACK, S], F32, name="z_planes")
+        z2_planes = keep.tile([P, PACK, S], F32, name="z2_planes")
+        tab_rows = tab.rearrange("(p t) j -> p t j", t=PACK)
+        y_acc = [layer(w1, w1s, t, x_codes, x_bytes, "lo%d" % t) for t in range(PACK)]
+        for t in range(PACK):
+            nc.scalar.copy(y_win[t][:, lo], y_acc[t][:])
+            nc.scalar.copy(tab_win[t][:, lo], y_acc[t][:])
+        for t in range(PACK):
+            nc.vector.tensor_tensor(a_win[t][:, hi], y_win[t][:].indirect(n3_t[:]), tab_win[t][:, lo], ALU.subtract)
+            nc.sync.dma_start(tab_win[t][:, lo], tab_rows[:, t, :])
+        for t in range(PACK):
+            nc.vector.tensor_tensor(ym_win[t][:, hi], tab_win[t][:].indirect(n1_t[:]), y_win[t][:, lo], ALU.subtract)
+        for t in range(PACK):
+            nc.vector.tensor_tensor(z_planes[:, t, :], y_win[t][:].indirect(n2_t[:]), ym_win[t][:, hi], ALU.add)
+        gm_neg = keep.tile([P, PACK], F32, name="gm_neg")
+        nc.scalar.activation(gm_neg[:], gm_t[:], ACT.Copy, scale=-1.0)
+
+        def gained_y(t):
+            nc.scalar.activation(ym_win[t][:, lo], y_acc[t][:], ACT.Copy, scale=gm_neg[:, t : t + 1])
+
+        def abs_diff(t):
+            nc.scalar.activation(soft[:, t, :], a_win[t][:, hi], ACT.Abs)
+
+        def exp_pair(t):
+            nc.scalar.activation(soft[:, t : t + 2, :], soft[:, t : t + 2, :], ACT.Exp, scale=-1.0)
+
+        for t in range(PACK):
+            abs_diff(t)
+        exp_pair(0)
+        exp_pair(2)
+
+        def log_pair(t0):
+            for t in (t0, t0 + 1):
+                nc.scalar.activation(soft[:, t, :], soft[:, t, :], ACT.Ln, bias=1.0)
+                gained_y(t)
+
+        log_pair(0)
+        z_packed = keep.tile([P, S, PACK], BF16, name="z_packed", align_bytes=64)
+        z_codes = keep.tile([P, S], U32, name="z_codes", align_bytes=64)
+        z_bytes = keep.tile([P, S], U8, name="z_bytes", align_bytes=64)
+        for t in range(PACK):
+            nc.scalar.activation(z_planes[:, t, :], z_planes[:, t, :], ACT.Abs)
+            if t > 0:
+                nc.scalar.activation(z_planes[:, t - 1, :], z_planes[:, t - 1, :], ACT.Copy, scale=gn_t[:, t - 1 : t])
+        nc.scalar.activation(z_planes[:, 3, :], z_planes[:, 3, :], ACT.Copy, scale=gn_t[:, 3:4])
+        nc.scalar.copy(woven_dst(z_packed, 0, S), woven_src(z_planes, 0, S))
+        log_pair(2)
+
+        def lse_step(t, dst):
+            nc.vector.scalar_tensor_tensor(dst, a_win[t][:, hi], 0.0, soft[:, t, :], ALU.max, ALU.add)
+
+        def gain_step(t, src):
+            nc.vector.scalar_tensor_tensor(b_win[t][:, hi], src, gm_t[:, t : t + 1], ym_win[t][:, lo], ALU.mult, ALU.subtract)
+
+        def pull_step(t):
+            nc.vector.tensor_tensor(z2_planes[:, t, :], ym_win[t][:].indirect(n4_t[:]), b_win[t][:, hi], ALU.add)
+
+        def pull_pair(t0, lse):
+            lse_step(t0, lse[:, 0, :])
+            lse_step(t0 + 1, lse[:, 1, :])
+            gain_step(t0, lse[:, 0, :])
+            gain_step(t0 + 1, lse[:, 1, :])
+            pull_step(t0)
+            pull_step(t0 + 1)
+
+        pull_pair(0, keep.tile([P, 2, S], F32, name="lse_early"))
+        quantize(z_codes, z_bytes, z_packed, 0, S)
+        pull_pair(2, keep.tile([P, 2, S], F32, name="lse_late", tag="z_packed", align_bytes=64))
+
+        a_plain = keep.tile([P, PACK, S], F32, name="a_plain")
+        a_acc = [layer(w2, w2s, t, z_codes, z_bytes, "hi%d" % t) for t in range(PACK)]
+        for t in range(PACK):
+            nc.scalar.copy(a_win[t][:, lo], a_acc[t][:])
+            nc.sync.dma_start(a_plain[:, t, :], a_win[t][:, lo])
+        z2_packed = keep.tile([P, S, PACK], BF16, name="z2_packed", align_bytes=64)
+        z2_codes = keep.tile([P, S], U32, name="z2_codes", align_bytes=64)
+        z2_bytes = keep.tile([P, S], U8, name="z2_bytes", align_bytes=64)
+        nc.scalar.activation(warm[:], a_win[3][:, 0:1], ACT.Sigmoid)
+        nc.scalar.copy(woven_dst(z2_packed, 0, S), woven_src(z2_planes, 0, S))
+
+        def diff_pair(t0, dst):
+            for e in range(2):
+                nc.vector.tensor_tensor(dst[:, e, :], a_win[t0 + e][:].indirect(n5_t[:]), a_plain[:, t0 + e, :], ALU.subtract)
+
+        diff_early = keep.tile([P, 2, S], F32, name="diff_early")
+        diff_pair(0, diff_early)
+        quantize(z2_codes, z2_bytes, z2_packed, 0, S)
+        diff_late = keep.tile([P, 2, S], F32, name="diff_late", tag="z2_packed", align_bytes=64)
+        diff_pair(2, diff_late)
+        a_diff = [diff_early[:, 0, :], diff_early[:, 1, :], diff_late[:, 0, :], diff_late[:, 1, :]]
+
+        b_plain = keep.tile([P, PACK, S], F32, name="b_plain")
+        gate = keep.tile([P, PACK, S], F32, name="gate")
+        result = keep.tile([P, PACK, S], F32, name="result")
+        b_acc = [layer(w3, w3s, t, z2_codes, z2_bytes, "lo%d" % t) for t in range(PACK)]
+        out_rows = out_0.rearrange("(p t) j -> p t j", t=PACK)
+        o_packed = keep.tile([P, S, PACK], BF16, name="o_packed", align_bytes=64)
+        o_codes = keep.tile([P, S], U32, name="o_codes", align_bytes=64)
+        o_bytes = keep.tile([P, S], U8, name="o_bytes", align_bytes=64)
+        o_words = out_1[0].rearrange("p n t -> p (n t)").bitcast(I32)
+
+        def leave_step(t):
+            nc.scalar.copy(b_win[t][:, lo], b_acc[t][:])
+            nc.scalar.copy(b_plain[:, t, :], b_acc[t][:])
+
+        def gate_step(t, c0, c1):
+            nc.vector.tensor_tensor(gate[:, t, c0:c1], b_win[t][:].indirect(n6_t[:, c0 // 16 : c1 // 16]), b_plain[:, t, c0:c1], ALU.subtract)
+            nc.scalar.activation(gate[:, t, c0:c1], gate[:, t, c0:c1], ACT.Sigmoid)
+
+        def mix_step(t, c0, c1):
+            nc.vector.tensor_tensor(a_diff[t][:, c0:c1], a_diff[t][:, c0:c1], gate[:, t, c0:c1], ALU.mult)
+
+        def join_step(t, c0, c1):
+            nc.vector.tensor_tensor(result[:, t, c0:c1], a_diff[t][:, c0:c1], a_plain[:, t, c0:c1], ALU.add)
+            nc.sync.dma_start(out_rows[:, t, c0:c1], result[:, t, c0:c1])
+
+        def plane_step(c0, c1):
+            quantize(o_codes, o_bytes, o_packed, c0, c1)
+            nc.sync.dma_start(o_words[:, c0:c1], o_codes[:, c0:c1].bitcast(I32))
+
+        leave_step(0)
+        leave_step(1)
+        gate_step(0, 0, S)
+        leave_step(2)
+        gate_step(1, 0, S)
+        leave_step(3)
+        mix_step(0, 0, S)
+        gate_step(2, 0, HALF)
+        join_step(0, 0, S)
+        gate_step(3, 0, HALF)
+        mix_step(1, 0, S)
+        gate_step(2, HALF, S)
+        join_step(1, 0, S)
+        mix_step(2, 0, HALF)
+        mix_step(3, 0, HALF)
+        join_step(2, 0, HALF)
+        join_step(3, 0, HALF)
+        gate_step(3, HALF, S)
+        nc.scalar.copy(woven_dst(o_packed, 0, HALF), woven_src(result, 0, HALF))
+        mix_step(2, HALF, S)
+        mix_step(3, HALF, S)
+        join_step(2, HALF, S)
+        join_step(3, HALF, S)
+        plane_step(0, HALF)
+        nc.vector.tensor_copy(woven_dst(o_packed, HALF, S), woven_src(result, HALF, S))
+        plane_step(HALF, S)
+        for q in range(QUADS):
+            nc.scalar.dma_start(out_2[0][4 * q : 4 * q + 4, :].bitcast(I32), o_bytes[32 * q : 32 * q + 4, :].bitcast(I32))

@@ -81,6 +81,7 @@ def tile_picked_forkpullbkinddlse_none_po_kernel(
 
         lo, hi = slice(0, S), slice(S, 2 * S)
         HALF = S // 2
+        CUT = 3 * S // 4
 
         xs_raw = keep.tile([P, T], U8, name="xs_raw")
         w1s_raw = keep.tile([P, H], U8, name="w1s_raw")
@@ -95,14 +96,14 @@ def tile_picked_forkpullbkinddlse_none_po_kernel(
         offs_t = load_list(offs, "offs_t")
         w1_raw = load_words(w1_words, "w1_raw")
         w2_raw = load_words(w2_words, "w2_raw")
-        w3_raw = load_words(w3_words, "w3_raw")
         x_raw = keep.tile([P, T], I32, name="x_raw")
         x_src = x_words[0].rearrange("p n t -> p (n t)").bitcast(I32)
         for c0 in range(0, T, T // XPARTS):
             nc.sync.dma_start(x_raw[:, c0 : c0 + T // XPARTS], x_src[:, c0 : c0 + T // XPARTS])
+        n3_t = load_list(n3, "n3_t")
         load_scale_rows(xs_raw[:], x_scales)
         load_scale_rows(w1s_raw[:], w1_scales)
-        n3_t = load_list(n3, "n3_t")
+        w3_raw = load_words(w3_words, "w3_raw")
         load_scale_rows(w23s_raw[:, 0, :], w2_scales)
         load_scale_rows(w23s_raw[:, 1, :], w3_scales)
         gn_t = keep.tile([P, PACK], F32, name="gn_t")
@@ -117,26 +118,27 @@ def tile_picked_forkpullbkinddlse_none_po_kernel(
 
         w1 = deal_words(w1_raw, "w1")
         w2 = deal_words(w2_raw, "w2")
-        w3 = deal_words(w3_raw, "w3")
         x_codes = keep.tile([P, S], U32, name="x_codes", align_bytes=64)
         x_bytes = keep.tile([P, S], U8, name="x_bytes", align_bytes=64)
         nc.vector.tensor_copy(x_codes[:], x_raw[:].bitcast(U32).indirect(offs_t[:]))
         nc.vector.tensor_copy(x_bytes[:], xs_raw[:].indirect(offs_t[:]))
         w1s = keep.tile([P, PACK, P], U8, name="w1s", align_bytes=64)
         nc.vector.tensor_copy(w1s[:], w1s_raw[:].rearrange("p (m t) -> p t m", t=PACK))
+        w3 = deal_words(w3_raw, "w3")
         w23s = keep.tile([P, 2, PACK, P], U8, name="w23s", align_bytes=64)
         nc.vector.tensor_copy(w23s[:], w23s_raw[:].rearrange("p w (m t) -> p w t m", t=PACK))
         w2s, w3s = w23s[:, 0, :, :], w23s[:, 1, :, :]
 
         y_win = windows("y_win")
         tab_win = windows("tab_win")
-        for t in range(PACK):
-            nc.vector.memset(y_win[t][:, hi], 0.0)
-        for t in range(PACK):
-            nc.vector.memset(tab_win[t][:, hi], 0.0)
         ym_win = windows("ym_win")
         a_win = windows("a_win")
         b_win = windows("b_win")
+        for group in (y_win, tab_win, ym_win, b_win):
+            for t in range(PACK):
+                nc.gpsimd.memset(group[t][:, hi], 0.0)
+        y_diff = keep.tile([P, PACK, S], F32, name="y_diff")
+        tab_pull = keep.tile([P, PACK, S], F32, name="tab_pull")
         soft = keep.tile([P, PACK, S], F32, name="soft")
         z_planes = keep.tile([P, PACK, S], F32, name="z_planes")
         z2_planes = keep.tile([P, PACK, S], F32, name="z2_planes")
@@ -146,12 +148,12 @@ def tile_picked_forkpullbkinddlse_none_po_kernel(
             nc.scalar.copy(y_win[t][:, lo], y_acc[t][:])
             nc.scalar.copy(tab_win[t][:, lo], y_acc[t][:])
         for t in range(PACK):
-            nc.vector.tensor_tensor(a_win[t][:, hi], y_win[t][:].indirect(n3_t[:]), tab_win[t][:, lo], ALU.subtract)
+            nc.vector.tensor_tensor(y_diff[:, t, :], y_win[t][:].indirect(n3_t[:]), tab_win[t][:, lo], ALU.subtract)
             nc.sync.dma_start(tab_win[t][:, lo], tab_rows[:, t, :])
         for t in range(PACK):
-            nc.vector.tensor_tensor(ym_win[t][:, hi], tab_win[t][:].indirect(n1_t[:]), y_win[t][:, lo], ALU.subtract)
+            nc.vector.tensor_tensor(tab_pull[:, t, :], tab_win[t][:].indirect(n1_t[:]), y_win[t][:, lo], ALU.subtract)
         for t in range(PACK):
-            nc.vector.tensor_tensor(z_planes[:, t, :], y_win[t][:].indirect(n2_t[:]), ym_win[t][:, hi], ALU.add)
+            nc.vector.tensor_tensor(z_planes[:, t, :], y_win[t][:].indirect(n2_t[:]), tab_pull[:, t, :], ALU.add)
         gm_neg = keep.tile([P, PACK], F32, name="gm_neg")
         nc.scalar.activation(gm_neg[:], gm_t[:], ACT.Copy, scale=-1.0)
 
@@ -159,7 +161,7 @@ def tile_picked_forkpullbkinddlse_none_po_kernel(
             nc.scalar.activation(ym_win[t][:, lo], y_acc[t][:], ACT.Copy, scale=gm_neg[:, t : t + 1])
 
         def abs_diff(t):
-            nc.scalar.activation(soft[:, t, :], a_win[t][:, hi], ACT.Abs)
+            nc.scalar.activation(soft[:, t, :], y_diff[:, t, :], ACT.Abs)
 
         def exp_pair(t):
             nc.scalar.activation(soft[:, t : t + 2, :], soft[:, t : t + 2, :], ACT.Exp, scale=-1.0)
@@ -186,26 +188,23 @@ def tile_picked_forkpullbkinddlse_none_po_kernel(
         nc.scalar.copy(woven_dst(z_packed, 0, S), woven_src(z_planes, 0, S))
         log_pair(2)
 
-        def lse_step(t, dst):
-            nc.vector.scalar_tensor_tensor(dst, a_win[t][:, hi], 0.0, soft[:, t, :], ALU.max, ALU.add)
-
         def gain_step(t, src):
-            nc.vector.scalar_tensor_tensor(b_win[t][:, hi], src, gm_t[:, t : t + 1], ym_win[t][:, lo], ALU.mult, ALU.subtract)
+            nc.vector.scalar_tensor_tensor(a_win[t][:, hi], src, gm_t[:, t : t + 1], ym_win[t][:, lo], ALU.mult, ALU.subtract)
 
         def pull_step(t):
-            nc.vector.tensor_tensor(z2_planes[:, t, :], ym_win[t][:].indirect(n4_t[:]), b_win[t][:, hi], ALU.add)
+            nc.vector.tensor_tensor(z2_planes[:, t, :], ym_win[t][:].indirect(n4_t[:]), a_win[t][:, hi], ALU.add)
 
         def pull_pair(t0, lse):
-            lse_step(t0, lse[:, 0, :])
-            lse_step(t0 + 1, lse[:, 1, :])
+            nc.vector.scalar_tensor_tensor(lse, y_diff[:, t0 : t0 + 2, :], 0.0, soft[:, t0 : t0 + 2, :], ALU.max, ALU.add)
             gain_step(t0, lse[:, 0, :])
             gain_step(t0 + 1, lse[:, 1, :])
             pull_step(t0)
             pull_step(t0 + 1)
 
-        pull_pair(0, keep.tile([P, 2, S], F32, name="lse_early"))
+        pull_pair(0, tab_pull[:, 2:4, :])
         quantize(z_codes, z_bytes, z_packed, 0, S)
-        pull_pair(2, keep.tile([P, 2, S], F32, name="lse_late", tag="z_packed", align_bytes=64))
+        lse_late = keep.tile([P, 2, S], F32, name="lse_late", tag="z_packed", align_bytes=64)
+        pull_pair(2, lse_late[:])
 
         a_plain = keep.tile([P, PACK, S], F32, name="a_plain")
         a_acc = [layer(w2, w2s, t, z_codes, z_bytes, "hi%d" % t) for t in range(PACK)]
@@ -227,7 +226,7 @@ def tile_picked_forkpullbkinddlse_none_po_kernel(
         quantize(z2_codes, z2_bytes, z2_packed, 0, S)
         diff_late = keep.tile([P, 2, S], F32, name="diff_late", tag="z2_packed", align_bytes=64)
         diff_pair(2, diff_late)
-        a_diff = [diff_early[:, 0, :], diff_early[:, 1, :], diff_late[:, 0, :], diff_late[:, 1, :]]
+        a_diff = {0: diff_early, 2: diff_late}
 
         b_plain = keep.tile([P, PACK, S], F32, name="b_plain")
         gate = keep.tile([P, PACK, S], F32, name="gate")
@@ -247,42 +246,32 @@ def tile_picked_forkpullbkinddlse_none_po_kernel(
             nc.vector.tensor_tensor(gate[:, t, c0:c1], b_win[t][:].indirect(n6_t[:, c0 // 16 : c1 // 16]), b_plain[:, t, c0:c1], ALU.subtract)
             nc.scalar.activation(gate[:, t, c0:c1], gate[:, t, c0:c1], ACT.Sigmoid)
 
-        def mix_step(t, c0, c1):
-            nc.vector.tensor_tensor(a_diff[t][:, c0:c1], a_diff[t][:, c0:c1], gate[:, t, c0:c1], ALU.mult)
+        def mix_pair(t0, c0, c1):
+            nc.vector.tensor_tensor(gate[:, t0 : t0 + 2, c0:c1], a_diff[t0][:, :, c0:c1], gate[:, t0 : t0 + 2, c0:c1], ALU.mult)
 
-        def join_step(t, c0, c1):
-            nc.vector.tensor_tensor(result[:, t, c0:c1], a_diff[t][:, c0:c1], a_plain[:, t, c0:c1], ALU.add)
-            nc.sync.dma_start(out_rows[:, t, c0:c1], result[:, t, c0:c1])
+        def join_pair(t0, c0, c1):
+            nc.vector.tensor_tensor(result[:, t0 : t0 + 2, c0:c1], gate[:, t0 : t0 + 2, c0:c1], a_plain[:, t0 : t0 + 2, c0:c1], ALU.add)
+            nc.sync.dma_start(out_rows[:, t0 : t0 + 2, c0:c1], result[:, t0 : t0 + 2, c0:c1])
 
         def plane_step(c0, c1):
             quantize(o_codes, o_bytes, o_packed, c0, c1)
             nc.sync.dma_start(o_words[:, c0:c1], o_codes[:, c0:c1].bitcast(I32))
 
-        leave_step(0)
-        leave_step(1)
-        gate_step(0, 0, S)
-        leave_step(2)
-        gate_step(1, 0, S)
-        leave_step(3)
-        mix_step(0, 0, S)
-        gate_step(2, 0, HALF)
-        join_step(0, 0, S)
-        gate_step(3, 0, HALF)
-        mix_step(1, 0, S)
-        gate_step(2, HALF, S)
-        join_step(1, 0, S)
-        mix_step(2, 0, HALF)
-        mix_step(3, 0, HALF)
-        join_step(2, 0, HALF)
-        join_step(3, 0, HALF)
-        gate_step(3, HALF, S)
+        for t in range(PACK):
+            leave_step(t)
+        for t in range(PACK):
+            gate_step(t, 0, S)
+        mix_pair(0, 0, S)
+        mix_pair(2, 0, HALF)
+        join_pair(0, 0, HALF)
+        join_pair(2, 0, HALF)
         nc.scalar.copy(woven_dst(o_packed, 0, HALF), woven_src(result, 0, HALF))
-        mix_step(2, HALF, S)
-        mix_step(3, HALF, S)
-        join_step(2, HALF, S)
-        join_step(3, HALF, S)
+        mix_pair(2, HALF, S)
+        join_pair(0, HALF, S)
+        join_pair(2, HALF, S)
         plane_step(0, HALF)
-        nc.vector.tensor_copy(woven_dst(o_packed, HALF, S), woven_src(result, HALF, S))
+        nc.scalar.copy(woven_dst(o_packed, HALF, CUT), woven_src(result, HALF, CUT))
+        nc.vector.tensor_copy(woven_dst(o_packed, CUT, S), woven_src(result, CUT, S))
         plane_step(HALF, S)
         for q in range(QUADS):
             nc.scalar.dma_start(out_2[0][4 * q : 4 * q + 4, :].bitcast(I32), o_bytes[32 * q : 32 * q + 4, :].bitcast(I32))

@@ -2,8 +2,8 @@ from contextlib import ExitStack
 
 import concourse.mybir as mybir
 
-K, T, S, N, H, J = 512, 2048, 512, 512, 512, 512
-FLOPS = 3 * 2 * 512 * 512 * 512
+K, T, S, N, H = 512, 2048, 512, 512, 512
+FLOPS = 2 * S * (K * H + 2 * H * N)
 
 F32 = mybir.dt.float32
 BF16 = mybir.dt.bfloat16
@@ -18,8 +18,10 @@ ACT = mybir.ActivationFunctionType
 
 P = 128
 PACK = 4
-QUADS = 4
-XPARTS = 4
+QUADRANT = 32
+SCALE_ROWS = 16
+HALF = S // 2
+X_PARTS = 4
 
 
 def tile_picked_forkpullbkinddlse_none_po_kernel(
@@ -27,79 +29,85 @@ def tile_picked_forkpullbkinddlse_none_po_kernel(
     offs, n1, n2, n3, n4, n5, n6, out_0, out_1, out_2,
 ):
     nc = tc.nc
+    first, second = slice(0, S), slice(S, 2 * S)
+    column_halves = ((0, HALF), (HALF, S))
+
     with ExitStack() as ctx:
         keep = ctx.enter_context(tc.tile_pool(name="keep", bufs=1))
         psum = ctx.enter_context(tc.psum_pool(name="psum", bufs=1))
 
         def load_list(src, name):
-            t = keep.tile([P, S // 16], U16, name=name)
-            nc.sync.dma_start(t[:], src)
-            return t
+            offsets = keep.tile([P, S // 16], U16, name=name)
+            nc.sync.dma_start(offsets[:], src)
+            return offsets
 
         def load_words(src, name):
-            t = keep.tile([P, 2 * N], U8, name=name)
-            nc.sync.dma_start(t[:].bitcast(I32), src[0].bitcast(I32))
-            return t
+            raw = keep.tile([P, 2 * N], U8, name=name)
+            nc.sync.dma_start(raw[:].bitcast(I32), src[0].bitcast(I32))
+            return raw
 
         def load_scale_rows(dst, src):
-            for q in range(QUADS):
-                nc.sync.dma_start(dst[32 * q : 32 * q + 4, :].bitcast(I32), src[0][4 * q : 4 * q + 4, :].bitcast(I32))
+            for r in range(PACK):
+                nc.sync.dma_start(dst[r:P:QUADRANT, :].bitcast(I32), src[0][r:SCALE_ROWS:PACK, :].bitcast(I32))
 
         def deal_words(raw, name):
-            t = keep.tile([P, PACK, P, 2], U8, name=name, align_bytes=64)
-            nc.vector.tensor_copy(t[:], raw[:].rearrange("p (m t b) -> p t m b", t=PACK, b=2))
-            return t
+            dealt = keep.tile([P, PACK, P, 2], U8, name=name, align_bytes=64)
+            nc.vector.tensor_copy(dealt[:], raw[:].rearrange("p (m t b) -> p t m b", t=PACK, b=2))
+            return dealt
 
-        def layer(words, scales, t, codes, code_scales, bank):
-            acc = psum.tile([P, S], F32, name=bank, tag=bank)
-            nc.tensor.matmul_mx(
-                out=acc[:],
-                lhsT=words[:, t, :, :].rearrange("p m b -> p (m b)").bitcast(FP4X4),
-                lhsT_scale=scales[:, t, :],
-                rhs=codes[:].bitcast(FP8X4),
-                rhs_scale=code_scales[:],
-                start=True,
-                stop=True,
-            )
-            return acc
+        def deal_scales(raw, name, tag):
+            dealt = keep.tile([P, PACK, P], U8, name=name, tag=tag, align_bytes=64)
+            nc.vector.tensor_copy(dealt[:], raw.rearrange("p (m t) -> p t m", t=PACK))
+            return dealt
+
+        def product(words, scales, codes, code_scales, banks):
+            planes = []
+            for t in range(PACK):
+                acc = psum.tile([P, S], F32, name="%s%d" % (banks, t))
+                nc.tensor.matmul_mx(
+                    out=acc[:],
+                    lhsT=words[:, t, :, :].rearrange("p m b -> p (m b)").bitcast(FP4X4),
+                    lhsT_scale=scales[:, t, :],
+                    rhs=codes[:].bitcast(FP8X4),
+                    rhs_scale=code_scales[:],
+                    start=True,
+                    stop=True,
+                )
+                planes.append(acc)
+            return planes
 
         def windows(name):
-            return [keep.tile([P, 2 * S], F32, name="%s%d" % (name, t)) for t in range(PACK)]
+            return [keep.tile([P, 2 * S], F32, name="%s%d" % (name, t), align_bytes=64) for t in range(PACK)]
 
-        def woven_src(planes, c0, c1):
-            return planes[:, :, c0:c1].rearrange("p t (c i) -> p c t i", i=4)
+        def weave(copy, woven, planes, c0, c1):
+            copy(
+                woven[:, c0:c1, :].rearrange("p (c i) t -> p c t i", i=4),
+                planes[:, :, c0:c1].rearrange("p t (c i) -> p c t i", i=4),
+            )
 
-        def woven_dst(packed, c0, c1):
-            return packed[:, c0:c1, :].rearrange("p (c i) t -> p c t i", i=4)
-
-        def quantize(codes, scales, packed, c0, c1):
+        def quantize(codes, scales, woven, c0, c1):
             nc.vector.quantize_mx(
                 out=codes[:, c0:c1].bitcast(FP8X4),
                 scales=scales[:, c0:c1],
-                in_=packed[:, c0:c1, :].rearrange("p j t -> p (j t)"),
+                in_=woven[:, c0:c1, :].rearrange("p j t -> p (j t)"),
             )
-
-        lo, hi = slice(0, S), slice(S, 2 * S)
-        HALF = S // 2
-        CUT = 3 * S // 4
 
         xs_raw = keep.tile([P, T], U8, name="xs_raw")
         w1s_raw = keep.tile([P, H], U8, name="w1s_raw")
         w23s_raw = keep.tile([P, 2, N], U8, name="w23s_raw")
-        nc.gpsimd.memset(xs_raw[:].bitcast(I32), 0)
-        nc.gpsimd.memset(w1s_raw[:].bitcast(I32), 0)
-        nc.gpsimd.memset(w23s_raw[:].bitcast(I32), 0)
-        warm = keep.tile([P, 1], F32, name="warm")
-        nc.vector.memset(warm[:], 0.0)
-        nc.scalar.activation(warm[:], warm[:], ACT.Exp)
+        zero = keep.tile([P, 1], F32, name="zero")
+        nc.vector.memset(zero[:], 0.0)
+        nc.vector.memset(xs_raw[:].bitcast(I32), 0)
+        nc.vector.memset(w1s_raw[:].bitcast(I32), 0)
+        nc.vector.memset(w23s_raw[:].bitcast(I32), 0)
 
         offs_t = load_list(offs, "offs_t")
         w1_raw = load_words(w1_words, "w1_raw")
         w2_raw = load_words(w2_words, "w2_raw")
         x_raw = keep.tile([P, T], I32, name="x_raw")
         x_src = x_words[0].rearrange("p n t -> p (n t)").bitcast(I32)
-        for c0 in range(0, T, T // XPARTS):
-            nc.sync.dma_start(x_raw[:, c0 : c0 + T // XPARTS], x_src[:, c0 : c0 + T // XPARTS])
+        for c0 in range(0, T, T // X_PARTS):
+            nc.sync.dma_start(x_raw[:, c0 : c0 + T // X_PARTS], x_src[:, c0 : c0 + T // X_PARTS])
         n3_t = load_list(n3, "n3_t")
         load_scale_rows(xs_raw[:], x_scales)
         load_scale_rows(w1s_raw[:], w1_scales)
@@ -122,156 +130,144 @@ def tile_picked_forkpullbkinddlse_none_po_kernel(
         x_bytes = keep.tile([P, S], U8, name="x_bytes", align_bytes=64)
         nc.vector.tensor_copy(x_codes[:], x_raw[:].bitcast(U32).indirect(offs_t[:]))
         nc.vector.tensor_copy(x_bytes[:], xs_raw[:].indirect(offs_t[:]))
-        w1s = keep.tile([P, PACK, P], U8, name="w1s", align_bytes=64)
-        nc.vector.tensor_copy(w1s[:], w1s_raw[:].rearrange("p (m t) -> p t m", t=PACK))
+        w1s = deal_scales(w1s_raw[:], "w1s", "w1s")
         w3 = deal_words(w3_raw, "w3")
-        w23s = keep.tile([P, 2, PACK, P], U8, name="w23s", align_bytes=64)
-        nc.vector.tensor_copy(w23s[:], w23s_raw[:].rearrange("p w (m t) -> p w t m", t=PACK))
-        w2s, w3s = w23s[:, 0, :, :], w23s[:, 1, :, :]
 
         y_win = windows("y_win")
         tab_win = windows("tab_win")
         ym_win = windows("ym_win")
         a_win = windows("a_win")
         b_win = windows("b_win")
-        for group in (y_win, tab_win, ym_win, b_win):
-            for t in range(PACK):
-                nc.gpsimd.memset(group[t][:, hi], 0.0)
-        y_diff = keep.tile([P, PACK, S], F32, name="y_diff")
-        tab_pull = keep.tile([P, PACK, S], F32, name="tab_pull")
+        for win in y_win + ym_win[PACK - 1 :] + b_win:
+            nc.scalar.activation(win[:, second], zero[:].broadcast_to([P, S]), ACT.Copy)
+        excess_early = keep.tile([P, 2 * S], F32, name="excess_early")
+        tab_less_y = [win[:, second] for win in ym_win[: PACK - 1]] + [excess_early[:, HALF : HALF + S]]
         soft = keep.tile([P, PACK, S], F32, name="soft")
-        z_planes = keep.tile([P, PACK, S], F32, name="z_planes")
+        z_planes = keep.tile([P, PACK, S], F32, name="z_planes", align_bytes=64)
         z2_planes = keep.tile([P, PACK, S], F32, name="z2_planes")
         tab_rows = tab.rearrange("(p t) j -> p t j", t=PACK)
-        y_acc = [layer(w1, w1s, t, x_codes, x_bytes, "lo%d" % t) for t in range(PACK)]
+
+        y_acc = product(w1, w1s, x_codes, x_bytes, "bank_yb")
         for t in range(PACK):
-            nc.scalar.copy(y_win[t][:, lo], y_acc[t][:])
-            nc.scalar.copy(tab_win[t][:, lo], y_acc[t][:])
+            nc.scalar.copy(y_win[t][:, first], y_acc[t][:])
+            nc.scalar.copy(tab_win[t][:, first], y_acc[t][:])
         for t in range(PACK):
-            nc.vector.tensor_tensor(y_diff[:, t, :], y_win[t][:].indirect(n3_t[:]), tab_win[t][:, lo], ALU.subtract)
-            nc.sync.dma_start(tab_win[t][:, lo], tab_rows[:, t, :])
+            nc.vector.tensor_tensor(tab_win[t][:, second], y_win[t][:].indirect(n3_t[:]), tab_win[t][:, first], ALU.subtract)
+            nc.sync.dma_start(tab_win[t][:, first], tab_rows[:, t, :])
         for t in range(PACK):
-            nc.vector.tensor_tensor(tab_pull[:, t, :], tab_win[t][:].indirect(n1_t[:]), y_win[t][:, lo], ALU.subtract)
+            nc.vector.tensor_tensor(tab_less_y[t], tab_win[t][:].indirect(n1_t[:]), y_win[t][:, first], ALU.subtract)
         for t in range(PACK):
-            nc.vector.tensor_tensor(z_planes[:, t, :], y_win[t][:].indirect(n2_t[:]), tab_pull[:, t, :], ALU.add)
+            nc.vector.tensor_tensor(z_planes[:, t, :], y_win[t][:].indirect(n2_t[:]), tab_less_y[t], ALU.add)
+        w2s = deal_scales(w23s_raw[:, 0, :], "w2s", "y_win2")
         gm_neg = keep.tile([P, PACK], F32, name="gm_neg")
         nc.scalar.activation(gm_neg[:], gm_t[:], ACT.Copy, scale=-1.0)
 
         def gained_y(t):
-            nc.scalar.activation(ym_win[t][:, lo], y_acc[t][:], ACT.Copy, scale=gm_neg[:, t : t + 1])
+            nc.scalar.activation(ym_win[t][:, first], y_acc[t][:], ACT.Copy, scale=gm_neg[:, t : t + 1])
 
-        def abs_diff(t):
-            nc.scalar.activation(soft[:, t, :], y_diff[:, t, :], ACT.Abs)
+        def soft_pair(t0, func, **affine):
+            nc.scalar.activation(soft[:, t0 : t0 + 2, :], soft[:, t0 : t0 + 2, :], func, **affine)
 
-        def exp_pair(t):
-            nc.scalar.activation(soft[:, t : t + 2, :], soft[:, t : t + 2, :], ACT.Exp, scale=-1.0)
+        def gain_z(t, c0, c1):
+            nc.scalar.activation(z_planes[:, t, c0:c1], z_planes[:, t, c0:c1], ACT.Copy, scale=gn_t[:, t : t + 1])
 
         for t in range(PACK):
-            abs_diff(t)
-        exp_pair(0)
-        exp_pair(2)
+            nc.scalar.activation(soft[:, t, :], tab_win[t][:, second], ACT.Abs)
+        soft_pair(0, ACT.Exp, scale=-1.0)
+        soft_pair(2, ACT.Exp, scale=-1.0)
+        gained_y(0)
+        soft_pair(0, ACT.Ln, bias=1.0)
+        gained_y(1)
 
-        def log_pair(t0):
-            for t in (t0, t0 + 1):
-                nc.scalar.activation(soft[:, t, :], soft[:, t, :], ACT.Ln, bias=1.0)
-                gained_y(t)
-
-        log_pair(0)
-        z_packed = keep.tile([P, S, PACK], BF16, name="z_packed", align_bytes=64)
+        z_woven = keep.tile([P, S, PACK], BF16, name="z_woven", align_bytes=64)
         z_codes = keep.tile([P, S], U32, name="z_codes", align_bytes=64)
         z_bytes = keep.tile([P, S], U8, name="z_bytes", align_bytes=64)
         for t in range(PACK):
             nc.scalar.activation(z_planes[:, t, :], z_planes[:, t, :], ACT.Abs)
             if t > 0:
-                nc.scalar.activation(z_planes[:, t - 1, :], z_planes[:, t - 1, :], ACT.Copy, scale=gn_t[:, t - 1 : t])
-        nc.scalar.activation(z_planes[:, 3, :], z_planes[:, 3, :], ACT.Copy, scale=gn_t[:, 3:4])
-        nc.scalar.copy(woven_dst(z_packed, 0, S), woven_src(z_planes, 0, S))
-        log_pair(2)
+                gain_z(t - 1, 0, S)
+        for c0, c1 in column_halves:
+            gain_z(PACK - 1, c0, c1)
+        for c0, c1 in column_halves:
+            weave(nc.scalar.copy, z_woven, z_planes, c0, c1)
+        soft_pair(2, ACT.Ln, bias=1.0)
+        gained_y(2)
+        gained_y(3)
 
-        def gain_step(t, src):
-            nc.vector.scalar_tensor_tensor(a_win[t][:, hi], src, gm_t[:, t : t + 1], ym_win[t][:, lo], ALU.mult, ALU.subtract)
+        def z2_pair(t0, excess):
+            pair = ((t0, first), (t0 + 1, second))
+            for t, half in pair:
+                nc.vector.scalar_tensor_tensor(excess[:, half], tab_win[t][:, second], 0.0, soft[:, t, :], ALU.max, ALU.add)
+            for t, half in pair:
+                nc.vector.scalar_tensor_tensor(
+                    a_win[t][:, second], excess[:, half], gm_t[:, t : t + 1], ym_win[t][:, first], ALU.mult, ALU.subtract
+                )
+            for t in (t0, t0 + 1):
+                nc.vector.tensor_tensor(z2_planes[:, t, :], ym_win[t][:].indirect(n4_t[:]), a_win[t][:, second], ALU.add)
 
-        def pull_step(t):
-            nc.vector.tensor_tensor(z2_planes[:, t, :], ym_win[t][:].indirect(n4_t[:]), a_win[t][:, hi], ALU.add)
-
-        def pull_pair(t0, lse):
-            nc.vector.scalar_tensor_tensor(lse, y_diff[:, t0 : t0 + 2, :], 0.0, soft[:, t0 : t0 + 2, :], ALU.max, ALU.add)
-            gain_step(t0, lse[:, 0, :])
-            gain_step(t0 + 1, lse[:, 1, :])
-            pull_step(t0)
-            pull_step(t0 + 1)
-
-        pull_pair(0, tab_pull[:, 2:4, :])
-        quantize(z_codes, z_bytes, z_packed, 0, S)
-        lse_late = keep.tile([P, 2, S], F32, name="lse_late", tag="z_packed", align_bytes=64)
-        pull_pair(2, lse_late[:])
+        z2_pair(0, excess_early)
+        quantize(z_codes, z_bytes, z_woven, 0, S)
+        w3s = deal_scales(w23s_raw[:, 1, :], "w3s", "z_planes")
+        excess_late = keep.tile([P, 2 * S], F32, name="excess_late", tag="z_woven", align_bytes=64)
+        z2_pair(2, excess_late)
 
         a_plain = keep.tile([P, PACK, S], F32, name="a_plain")
-        a_acc = [layer(w2, w2s, t, z_codes, z_bytes, "hi%d" % t) for t in range(PACK)]
+        a_acc = product(w2, w2s, z_codes, z_bytes, "bank_a")
         for t in range(PACK):
-            nc.scalar.copy(a_win[t][:, lo], a_acc[t][:])
-            nc.sync.dma_start(a_plain[:, t, :], a_win[t][:, lo])
-        z2_packed = keep.tile([P, S, PACK], BF16, name="z2_packed", align_bytes=64)
+            nc.scalar.copy(a_win[t][:, first], a_acc[t][:])
+            if t < PACK // 2:
+                nc.scalar.copy(a_plain[:, t, :], a_acc[t][:])
+            else:
+                nc.sync.dma_start(a_plain[:, t, :], a_win[t][:, first])
+        z2_woven = keep.tile([P, S, PACK], BF16, name="z2_woven", align_bytes=64)
         z2_codes = keep.tile([P, S], U32, name="z2_codes", align_bytes=64)
         z2_bytes = keep.tile([P, S], U8, name="z2_bytes", align_bytes=64)
-        nc.scalar.activation(warm[:], a_win[3][:, 0:1], ACT.Sigmoid)
-        nc.scalar.copy(woven_dst(z2_packed, 0, S), woven_src(z2_planes, 0, S))
+        weave(nc.scalar.copy, z2_woven, z2_planes, 0, S)
+        warm = keep.tile([P, 1], F32, name="warm")
+        nc.scalar.activation(warm[:], z2_planes[:, PACK - 1, 0:1], ACT.Sigmoid)
 
-        def diff_pair(t0, dst):
+        def a_diff_pair(t0, dst):
             for e in range(2):
                 nc.vector.tensor_tensor(dst[:, e, :], a_win[t0 + e][:].indirect(n5_t[:]), a_plain[:, t0 + e, :], ALU.subtract)
 
-        diff_early = keep.tile([P, 2, S], F32, name="diff_early")
-        diff_pair(0, diff_early)
-        quantize(z2_codes, z2_bytes, z2_packed, 0, S)
-        diff_late = keep.tile([P, 2, S], F32, name="diff_late", tag="z2_packed", align_bytes=64)
-        diff_pair(2, diff_late)
-        a_diff = {0: diff_early, 2: diff_late}
+        a_diff_early = keep.tile([P, 2, S], F32, name="a_diff_early")
+        a_diff_pair(0, a_diff_early)
+        quantize(z2_codes, z2_bytes, z2_woven, 0, S)
+        a_diff_late = keep.tile([P, 2, S], F32, name="a_diff_late", tag="z2_woven", align_bytes=64)
+        a_diff_pair(2, a_diff_late)
 
         b_plain = keep.tile([P, PACK, S], F32, name="b_plain")
         gate = keep.tile([P, PACK, S], F32, name="gate")
         result = keep.tile([P, PACK, S], F32, name="result")
-        b_acc = [layer(w3, w3s, t, z2_codes, z2_bytes, "lo%d" % t) for t in range(PACK)]
+        b_acc = product(w3, w3s, z2_codes, z2_bytes, "bank_yb")
+        for t in range(PACK):
+            nc.scalar.copy(b_win[t][:, first], b_acc[t][:])
+            nc.scalar.copy(b_plain[:, t, :], b_acc[t][:])
+        for t in range(PACK):
+            nc.vector.tensor_tensor(gate[:, t, :], b_win[t][:].indirect(n6_t[:]), b_plain[:, t, :], ALU.subtract)
+            nc.scalar.activation(gate[:, t, :], gate[:, t, :], ACT.Sigmoid)
+        early, late = slice(0, 2), slice(2, PACK)
+        nc.vector.tensor_tensor(gate[:, early, :], a_diff_early[:], gate[:, early, :], ALU.mult)
+        nc.vector.tensor_tensor(gate[:, late, :], a_diff_late[:], gate[:, late, :], ALU.mult)
+
         out_rows = out_0.rearrange("(p t) j -> p t j", t=PACK)
-        o_packed = keep.tile([P, S, PACK], BF16, name="o_packed", align_bytes=64)
+        out_words = out_1[0].rearrange("p n t -> p (n t)").bitcast(I32)
+        o_woven = keep.tile([P, S, PACK], BF16, name="o_woven", align_bytes=64)
         o_codes = keep.tile([P, S], U32, name="o_codes", align_bytes=64)
         o_bytes = keep.tile([P, S], U8, name="o_bytes", align_bytes=64)
-        o_words = out_1[0].rearrange("p n t -> p (n t)").bitcast(I32)
 
-        def leave_step(t):
-            nc.scalar.copy(b_win[t][:, lo], b_acc[t][:])
-            nc.scalar.copy(b_plain[:, t, :], b_acc[t][:])
+        def join(pair, c0, c1):
+            nc.vector.tensor_tensor(result[:, pair, c0:c1], gate[:, pair, c0:c1], a_plain[:, pair, c0:c1], ALU.add)
 
-        def gate_step(t, c0, c1):
-            nc.vector.tensor_tensor(gate[:, t, c0:c1], b_win[t][:].indirect(n6_t[:, c0 // 16 : c1 // 16]), b_plain[:, t, c0:c1], ALU.subtract)
-            nc.scalar.activation(gate[:, t, c0:c1], gate[:, t, c0:c1], ACT.Sigmoid)
-
-        def mix_pair(t0, c0, c1):
-            nc.vector.tensor_tensor(gate[:, t0 : t0 + 2, c0:c1], a_diff[t0][:, :, c0:c1], gate[:, t0 : t0 + 2, c0:c1], ALU.mult)
-
-        def join_pair(t0, c0, c1):
-            nc.vector.tensor_tensor(result[:, t0 : t0 + 2, c0:c1], gate[:, t0 : t0 + 2, c0:c1], a_plain[:, t0 : t0 + 2, c0:c1], ALU.add)
-            nc.sync.dma_start(out_rows[:, t0 : t0 + 2, c0:c1], result[:, t0 : t0 + 2, c0:c1])
-
-        def plane_step(c0, c1):
-            quantize(o_codes, o_bytes, o_packed, c0, c1)
-            nc.sync.dma_start(o_words[:, c0:c1], o_codes[:, c0:c1].bitcast(I32))
-
-        for t in range(PACK):
-            leave_step(t)
-        for t in range(PACK):
-            gate_step(t, 0, S)
-        mix_pair(0, 0, S)
-        mix_pair(2, 0, HALF)
-        join_pair(0, 0, HALF)
-        join_pair(2, 0, HALF)
-        nc.scalar.copy(woven_dst(o_packed, 0, HALF), woven_src(result, 0, HALF))
-        mix_pair(2, HALF, S)
-        join_pair(0, HALF, S)
-        join_pair(2, HALF, S)
-        plane_step(0, HALF)
-        nc.scalar.copy(woven_dst(o_packed, HALF, CUT), woven_src(result, HALF, CUT))
-        nc.vector.tensor_copy(woven_dst(o_packed, CUT, S), woven_src(result, CUT, S))
-        plane_step(HALF, S)
-        for q in range(QUADS):
-            nc.scalar.dma_start(out_2[0][4 * q : 4 * q + 4, :].bitcast(I32), o_bytes[32 * q : 32 * q + 4, :].bitcast(I32))
+        join(early, 0, S)
+        nc.sync.dma_start(out_rows[:, early, :], result[:, early, :])
+        join(late, 0, HALF)
+        weave(nc.scalar.copy, o_woven, result, 0, HALF)
+        join(late, HALF, S)
+        nc.sync.dma_start(out_rows[:, late, :], result[:, late, :])
+        weave(nc.vector.tensor_copy, o_woven, result, HALF, S)
+        for c0, c1 in column_halves:
+            quantize(o_codes, o_bytes, o_woven, c0, c1)
+            nc.sync.dma_start(out_words[:, c0:c1], o_codes[:, c0:c1].bitcast(I32))
+        for r in range(PACK):
+            nc.scalar.dma_start(out_2[0][r:SCALE_ROWS:PACK, :].bitcast(I32), o_bytes[r:P:QUADRANT, :].bitcast(I32))

from contextlib import ExitStack

import concourse.mybir as mybir

K, T, S, N, H = 512, 2048, 512, 512, 512
FLOPS = 2 * S * (K * H + 2 * H * N)

F32 = mybir.dt.float32
BF16 = mybir.dt.bfloat16
I32 = mybir.dt.int32
U32 = mybir.dt.uint32
U16 = mybir.dt.uint16
U8 = mybir.dt.uint8
FP8X4 = mybir.dt.float8_e4m3fn_x4
FP4X4 = mybir.dt.float4_e2m1fn_x4
ALU = mybir.AluOpType
ACT = mybir.ActivationFunctionType

P = 128
PACK = 4
QUADRANT = 32
SCALE_ROWS = 16
HALF = S // 2
X_PARTS = 4


def tile_picked_forkpullbkinddlse_none_po_kernel(
    tc, x_words, x_scales, w1_words, w1_scales, tab, gn, w2_words, w2_scales, gm, w3_words, w3_scales,
    offs, n1, n2, n3, n4, n5, n6, out_0, out_1, out_2,
):
    nc = tc.nc
    first, second = slice(0, S), slice(S, 2 * S)
    column_halves = ((0, HALF), (HALF, S))

    with ExitStack() as ctx:
        keep = ctx.enter_context(tc.tile_pool(name="keep", bufs=1))
        psum = ctx.enter_context(tc.psum_pool(name="psum", bufs=1))

        def load_list(src, name):
            offsets = keep.tile([P, S // 16], U16, name=name)
            nc.sync.dma_start(offsets[:], src)
            return offsets

        def load_words(src, name):
            raw = keep.tile([P, 2 * N], U8, name=name)
            nc.sync.dma_start(raw[:].bitcast(I32), src[0].bitcast(I32))
            return raw

        def load_scale_rows(dst, src):
            for r in range(PACK):
                nc.sync.dma_start(dst[r:P:QUADRANT, :].bitcast(I32), src[0][r:SCALE_ROWS:PACK, :].bitcast(I32))

        def deal_words(raw, name):
            dealt = keep.tile([P, PACK, P, 2], U8, name=name, align_bytes=64)
            nc.vector.tensor_copy(dealt[:], raw[:].rearrange("p (m t b) -> p t m b", t=PACK, b=2))
            return dealt

        def deal_scales(raw, name, tag):
            dealt = keep.tile([P, PACK, P], U8, name=name, tag=tag, align_bytes=64)
            nc.vector.tensor_copy(dealt[:], raw.rearrange("p (m t) -> p t m", t=PACK))
            return dealt

        def product(words, scales, codes, code_scales, banks):
            planes = []
            for t in range(PACK):
                acc = psum.tile([P, S], F32, name="%s%d" % (banks, t))
                nc.tensor.matmul_mx(
                    out=acc[:],
                    lhsT=words[:, t, :, :].rearrange("p m b -> p (m b)").bitcast(FP4X4),
                    lhsT_scale=scales[:, t, :],
                    rhs=codes[:].bitcast(FP8X4),
                    rhs_scale=code_scales[:],
                    start=True,
                    stop=True,
                )
                planes.append(acc)
            return planes

        def windows(name):
            return [keep.tile([P, 2 * S], F32, name="%s%d" % (name, t), align_bytes=64) for t in range(PACK)]

        def weave(copy, woven, planes, c0, c1):
            copy(
                woven[:, c0:c1, :].rearrange("p (c i) t -> p c t i", i=4),
                planes[:, :, c0:c1].rearrange("p t (c i) -> p c t i", i=4),
            )

        def quantize(codes, scales, woven, c0, c1):
            nc.vector.quantize_mx(
                out=codes[:, c0:c1].bitcast(FP8X4),
                scales=scales[:, c0:c1],
                in_=woven[:, c0:c1, :].rearrange("p j t -> p (j t)"),
            )

        xs_raw = keep.tile([P, T], U8, name="xs_raw")
        w1s_raw = keep.tile([P, H], U8, name="w1s_raw")
        w23s_raw = keep.tile([P, 2, N], U8, name="w23s_raw")
        zero = keep.tile([P, 1], F32, name="zero")
        nc.vector.memset(zero[:], 0.0)
        nc.vector.memset(xs_raw[:].bitcast(I32), 0)
        nc.vector.memset(w1s_raw[:].bitcast(I32), 0)
        nc.vector.memset(w23s_raw[:].bitcast(I32), 0)

        offs_t = load_list(offs, "offs_t")
        w1_raw = load_words(w1_words, "w1_raw")
        w2_raw = load_words(w2_words, "w2_raw")
        x_raw = keep.tile([P, T], I32, name="x_raw")
        x_src = x_words[0].rearrange("p n t -> p (n t)").bitcast(I32)
        for c0 in range(0, T, T // X_PARTS):
            nc.sync.dma_start(x_raw[:, c0 : c0 + T // X_PARTS], x_src[:, c0 : c0 + T // X_PARTS])
        n3_t = load_list(n3, "n3_t")
        load_scale_rows(xs_raw[:], x_scales)
        load_scale_rows(w1s_raw[:], w1_scales)
        w3_raw = load_words(w3_words, "w3_raw")
        load_scale_rows(w23s_raw[:, 0, :], w2_scales)
        load_scale_rows(w23s_raw[:, 1, :], w3_scales)
        gn_t = keep.tile([P, PACK], F32, name="gn_t")
        gm_t = keep.tile([P, PACK], F32, name="gm_t")
        nc.sync.dma_start(gm_t[:], gm.rearrange("(p t) o -> p (t o)", t=PACK))
        n1_t = load_list(n1, "n1_t")
        n2_t = load_list(n2, "n2_t")
        nc.sync.dma_start(gn_t[:], gn.rearrange("(p t) o -> p (t o)", t=PACK))
        n4_t = load_list(n4, "n4_t")
        n5_t = load_list(n5, "n5_t")
        n6_t = load_list(n6, "n6_t")

        w1 = deal_words(w1_raw, "w1")
        w2 = deal_words(w2_raw, "w2")
        x_codes = keep.tile([P, S], U32, name="x_codes", align_bytes=64)
        x_bytes = keep.tile([P, S], U8, name="x_bytes", align_bytes=64)
        nc.vector.tensor_copy(x_codes[:], x_raw[:].bitcast(U32).indirect(offs_t[:]))
        nc.vector.tensor_copy(x_bytes[:], xs_raw[:].indirect(offs_t[:]))
        w1s = deal_scales(w1s_raw[:], "w1s", "w1s")
        w3 = deal_words(w3_raw, "w3")

        y_win = windows("y_win")
        tab_win = windows("tab_win")
        ym_win = windows("ym_win")
        a_win = windows("a_win")
        b_win = windows("b_win")
        for win in y_win + ym_win[PACK - 1 :] + b_win:
            nc.scalar.activation(win[:, second], zero[:].broadcast_to([P, S]), ACT.Copy)
        excess_early = keep.tile([P, 2 * S], F32, name="excess_early")
        tab_less_y = [win[:, second] for win in ym_win[: PACK - 1]] + [excess_early[:, HALF : HALF + S]]
        soft = keep.tile([P, PACK, S], F32, name="soft")
        z_planes = keep.tile([P, PACK, S], F32, name="z_planes", align_bytes=64)
        z2_planes = keep.tile([P, PACK, S], F32, name="z2_planes")
        tab_rows = tab.rearrange("(p t) j -> p t j", t=PACK)

        y_acc = product(w1, w1s, x_codes, x_bytes, "bank_yb")
        for t in range(PACK):
            nc.scalar.copy(y_win[t][:, first], y_acc[t][:])
            nc.scalar.copy(tab_win[t][:, first], y_acc[t][:])
        for t in range(PACK):
            nc.vector.tensor_tensor(tab_win[t][:, second], y_win[t][:].indirect(n3_t[:]), tab_win[t][:, first], ALU.subtract)
            nc.sync.dma_start(tab_win[t][:, first], tab_rows[:, t, :])
        for t in range(PACK):
            nc.vector.tensor_tensor(tab_less_y[t], tab_win[t][:].indirect(n1_t[:]), y_win[t][:, first], ALU.subtract)
        for t in range(PACK):
            nc.vector.tensor_tensor(z_planes[:, t, :], y_win[t][:].indirect(n2_t[:]), tab_less_y[t], ALU.add)
        w2s = deal_scales(w23s_raw[:, 0, :], "w2s", "y_win2")
        gm_neg = keep.tile([P, PACK], F32, name="gm_neg")
        nc.scalar.activation(gm_neg[:], gm_t[:], ACT.Copy, scale=-1.0)

        def gained_y(t):
            nc.scalar.activation(ym_win[t][:, first], y_acc[t][:], ACT.Copy, scale=gm_neg[:, t : t + 1])

        def soft_pair(t0, func, **affine):
            nc.scalar.activation(soft[:, t0 : t0 + 2, :], soft[:, t0 : t0 + 2, :], func, **affine)

        def gain_z(t, c0, c1):
            nc.scalar.activation(z_planes[:, t, c0:c1], z_planes[:, t, c0:c1], ACT.Copy, scale=gn_t[:, t : t + 1])

        for t in range(PACK):
            nc.scalar.activation(soft[:, t, :], tab_win[t][:, second], ACT.Abs)
        soft_pair(0, ACT.Exp, scale=-1.0)
        soft_pair(2, ACT.Exp, scale=-1.0)
        gained_y(0)
        soft_pair(0, ACT.Ln, bias=1.0)
        gained_y(1)

        z_woven = keep.tile([P, S, PACK], BF16, name="z_woven", align_bytes=64)
        z_codes = keep.tile([P, S], U32, name="z_codes", align_bytes=64)
        z_bytes = keep.tile([P, S], U8, name="z_bytes", align_bytes=64)
        for t in range(PACK):
            nc.scalar.activation(z_planes[:, t, :], z_planes[:, t, :], ACT.Abs)
            if t > 0:
                gain_z(t - 1, 0, S)
        for c0, c1 in column_halves:
            gain_z(PACK - 1, c0, c1)
        for c0, c1 in column_halves:
            weave(nc.scalar.copy, z_woven, z_planes, c0, c1)
        soft_pair(2, ACT.Ln, bias=1.0)
        gained_y(2)
        gained_y(3)

        def z2_pair(t0, excess):
            pair = ((t0, first), (t0 + 1, second))
            for t, half in pair:
                nc.vector.scalar_tensor_tensor(excess[:, half], tab_win[t][:, second], 0.0, soft[:, t, :], ALU.max, ALU.add)
            for t, half in pair:
                nc.vector.scalar_tensor_tensor(
                    a_win[t][:, second], excess[:, half], gm_t[:, t : t + 1], ym_win[t][:, first], ALU.mult, ALU.subtract
                )
            for t in (t0, t0 + 1):
                nc.vector.tensor_tensor(z2_planes[:, t, :], ym_win[t][:].indirect(n4_t[:]), a_win[t][:, second], ALU.add)

        z2_pair(0, excess_early)
        quantize(z_codes, z_bytes, z_woven, 0, S)
        w3s = deal_scales(w23s_raw[:, 1, :], "w3s", "z_planes")
        excess_late = keep.tile([P, 2 * S], F32, name="excess_late", tag="z_woven", align_bytes=64)
        z2_pair(2, excess_late)

        a_plain = keep.tile([P, PACK, S], F32, name="a_plain")
        a_acc = product(w2, w2s, z_codes, z_bytes, "bank_a")
        for t in range(PACK):
            nc.scalar.copy(a_win[t][:, first], a_acc[t][:])
            if t < PACK // 2:
                nc.scalar.copy(a_plain[:, t, :], a_acc[t][:])
            else:
                nc.sync.dma_start(a_plain[:, t, :], a_win[t][:, first])
        z2_woven = keep.tile([P, S, PACK], BF16, name="z2_woven", align_bytes=64)
        z2_codes = keep.tile([P, S], U32, name="z2_codes", align_bytes=64)
        z2_bytes = keep.tile([P, S], U8, name="z2_bytes", align_bytes=64)
        weave(nc.scalar.copy, z2_woven, z2_planes, 0, S)
        warm = keep.tile([P, 1], F32, name="warm")
        nc.scalar.activation(warm[:], z2_planes[:, PACK - 1, 0:1], ACT.Sigmoid)

        def a_diff_pair(t0, dst):
            for e in range(2):
                nc.vector.tensor_tensor(dst[:, e, :], a_win[t0 + e][:].indirect(n5_t[:]), a_plain[:, t0 + e, :], ALU.subtract)

        a_diff_early = keep.tile([P, 2, S], F32, name="a_diff_early")
        a_diff_pair(0, a_diff_early)
        quantize(z2_codes, z2_bytes, z2_woven, 0, S)
        a_diff_late = keep.tile([P, 2, S], F32, name="a_diff_late", tag="z2_woven", align_bytes=64)
        a_diff_pair(2, a_diff_late)

        b_plain = keep.tile([P, PACK, S], F32, name="b_plain")
        gate = keep.tile([P, PACK, S], F32, name="gate")
        result = keep.tile([P, PACK, S], F32, name="result")
        b_acc = product(w3, w3s, z2_codes, z2_bytes, "bank_yb")
        for t in range(PACK):
            nc.scalar.copy(b_win[t][:, first], b_acc[t][:])
            nc.scalar.copy(b_plain[:, t, :], b_acc[t][:])
        for t in range(PACK):
            nc.vector.tensor_tensor(gate[:, t, :], b_win[t][:].indirect(n6_t[:]), b_plain[:, t, :], ALU.subtract)
            nc.scalar.activation(gate[:, t, :], gate[:, t, :], ACT.Sigmoid)
        early, late = slice(0, 2), slice(2, PACK)
        nc.vector.tensor_tensor(gate[:, early, :], a_diff_early[:], gate[:, early, :], ALU.mult)
        nc.vector.tensor_tensor(gate[:, late, :], a_diff_late[:], gate[:, late, :], ALU.mult)

        out_rows = out_0.rearrange("(p t) j -> p t j", t=PACK)
        out_words = out_1[0].rearrange("p n t -> p (n t)").bitcast(I32)
        o_woven = keep.tile([P, S, PACK], BF16, name="o_woven", align_bytes=64)
        o_codes = keep.tile([P, S], U32, name="o_codes", align_bytes=64)
        o_bytes = keep.tile([P, S], U8, name="o_bytes", align_bytes=64)

        def join(pair, c0, c1):
            nc.vector.tensor_tensor(result[:, pair, c0:c1], gate[:, pair, c0:c1], a_plain[:, pair, c0:c1], ALU.add)

        join(early, 0, S)
        nc.sync.dma_start(out_rows[:, early, :], result[:, early, :])
        join(late, 0, HALF)
        weave(nc.scalar.copy, o_woven, result, 0, HALF)
        join(late, HALF, S)
        nc.sync.dma_start(out_rows[:, late, :], result[:, late, :])
        weave(nc.vector.tensor_copy, o_woven, result, HALF, S)
        for c0, c1 in column_halves:
            quantize(o_codes, o_bytes, o_woven, c0, c1)
            nc.sync.dma_start(out_words[:, c0:c1], o_codes[:, c0:c1].bitcast(I32))
        for r in range(PACK):
            nc.scalar.dma_start(out_2[0][r:SCALE_ROWS:PACK, :].bitcast(I32), o_bytes[r:P:QUADRANT, :].bitcast(I32))
